import numpy as np
import ml_dtypes

BF16 = ml_dtypes.bfloat16


def bf(x):
    return np.asarray(x, np.float32).astype(BF16)


def f32(x):
    return np.asarray(x, np.float32)


def f64(x):
    return np.asarray(x).astype(np.float64)


def striped(idx):
    return np.tile(idx.reshape(-1, 16).T, (8, 1))


def rows(idx, k):
    return np.tile(idx, (k, 1))


def look(tab, idx):
    return np.take_along_axis(f64(tab), rows(idx, len(tab)), axis=1)


K, S, D, V, N = 128, 2048, 2, 1024, 2048


def setup_inputs():
    return {"tab": f32(np.random.standard_normal((K, S))), "u0": f32(np.random.uniform(0.2, 1.0, (K, V))), "u1": f32(np.random.uniform(0.2, 1.0, (K, V))), "offs": striped(np.random.permutation(S)[:N])}


def reference(tab, u0, u1, offs):
    idx = offs[:16].T.reshape(-1)
    x = f64(u0) * np.minimum(np.maximum(look(tab, idx[:V]), -1.25), 1.0) + f64(u1) * np.minimum(np.maximum(look(tab, idx[1 * V:2 * V]), -1.25), 1.0)
    return x

@@ -1,0 +1,34 @@
+import concourse.mybir as mybir
+
+FLOPS = 128 * 1024 * 7
+LOW, HIGH = -1.25, 1.0
+
+
+def tile_lookup_clipmix_out_kernel(tc, tab, u0, u1, offs, out):
+    nc = tc.nc
+    F32, U16 = mybir.dt.float32, mybir.dt.uint16
+    alu = mybir.AluOpType
+    rows, table_columns = tab.shape
+    n = out.shape[1]
+    offset_columns = n // 16
+
+    with tc.tile_pool(name="held", bufs=1) as held:
+        offsets = held.tile([rows, offs.shape[1]], U16, name="offsets")
+        nc.sync.dma_start(offsets[:], offs)
+        table = held.tile([rows, table_columns], F32, name="table")
+        nc.scalar.dma_start(table[:], tab)
+
+        products = []
+        for d, u in enumerate((u0, u1)):
+            weights = held.tile([rows, n], F32, name="weights%d" % d)
+            nc.sync.dma_start(weights[:], u)
+            entries = offsets[:, d * offset_columns : (d + 1) * offset_columns]
+            clamped = held.tile([rows, n], F32, name="clamped%d" % d)
+            nc.vector.tensor_scalar(clamped[:], table[:].indirect(entries), LOW, HIGH, alu.max, alu.min)
+            product = held.tile([rows, n], F32, name="product%d" % d)
+            nc.vector.tensor_tensor(product[:], clamped[:], weights[:], alu.mult)
+            products.append(product)
+
+        total = held.tile([rows, n], F32, name="total")
+        nc.vector.tensor_tensor(total[:], products[0][:], products[1][:], alu.add)
+        nc.sync.dma_start(out, total[:])

@@ -10,25 +10,36 @@ def tile_lookup_clipmix_out_kernel(tc, tab, u0, u1, offs, out):
     alu = mybir.AluOpType
     rows, table_columns = tab.shape
     n = out.shape[1]
-    offset_columns = n // 16
 
     with tc.tile_pool(name="held", bufs=1) as held:
         offsets = held.tile([rows, offs.shape[1]], U16, name="offsets")
-        nc.sync.dma_start(offsets[:], offs)
         table = held.tile([rows, table_columns], F32, name="table")
+        weights0 = held.tile([rows, n], F32, name="weights0")
+        weights1 = held.tile([rows, n], F32, name="weights1")
+        nc.sync.dma_start(offsets[:], offs)
         nc.scalar.dma_start(table[:], tab)
+        nc.sync.dma_start(weights0[:], u0)
+        nc.sync.dma_start(weights1[:], u1)
 
-        products = []
-        for d, u in enumerate((u0, u1)):
-            weights = held.tile([rows, n], F32, name="weights%d" % d)
-            nc.sync.dma_start(weights[:], u)
-            entries = offsets[:, d * offset_columns : (d + 1) * offset_columns]
-            clamped = held.tile([rows, n], F32, name="clamped%d" % d)
-            nc.vector.tensor_scalar(clamped[:], table[:].indirect(entries), LOW, HIGH, alu.max, alu.min)
-            product = held.tile([rows, n], F32, name="product%d" % d)
-            nc.vector.tensor_tensor(product[:], clamped[:], weights[:], alu.mult)
-            products.append(product)
-
+        clamped0 = held.tile([rows, n], F32, name="clamped0")
+        clamped1 = held.tile([rows, n], F32, name="clamped1")
+        product0 = held.tile([rows, n], F32, name="product0")
+        product1 = held.tile([rows, n], F32, name="product1")
         total = held.tile([rows, n], F32, name="total")
-        nc.vector.tensor_tensor(total[:], products[0][:], products[1][:], alu.add)
+
+        width = n // 2
+        halves = (slice(0, width), slice(width, n))
+
+        for half in halves:
+            entries = offsets[:, half.start // 16 : half.stop // 16]
+            nc.vector.tensor_scalar(clamped0[:, half], table[:].indirect(entries), LOW, HIGH, alu.max, alu.min)
+            nc.gpsimd.tensor_tensor(product0[:, half], clamped0[:, half], weights0[:, half], alu.mult)
+
+        for half in halves:
+            entries = offsets[:, (n + half.start) // 16 : (n + half.stop) // 16]
+            nc.vector.tensor_scalar(clamped1[:, half], table[:].indirect(entries), LOW, HIGH, alu.max, alu.min)
+        for half in halves:
+            nc.vector.tensor_tensor(product1[:, half], clamped1[:, half], weights1[:, half], alu.mult)
+        for half in halves:
+            nc.vector.tensor_tensor(total[:, half], product0[:, half], product1[:, half], alu.add)
         nc.sync.dma_start(out, total[:])

import concourse.mybir as mybir

FLOPS = 128 * 1024 * 7
LOW, HIGH = -1.25, 1.0


def tile_lookup_clipmix_out_kernel(tc, tab, u0, u1, offs, out):
    nc = tc.nc
    F32, U16 = mybir.dt.float32, mybir.dt.uint16
    alu = mybir.AluOpType
    rows, table_columns = tab.shape
    n = out.shape[1]

    with tc.tile_pool(name="held", bufs=1) as held:
        offsets = held.tile([rows, offs.shape[1]], U16, name="offsets")
        table = held.tile([rows, table_columns], F32, name="table")
        weights0 = held.tile([rows, n], F32, name="weights0")
        weights1 = held.tile([rows, n], F32, name="weights1")
        nc.sync.dma_start(offsets[:], offs)
        nc.scalar.dma_start(table[:], tab)
        nc.sync.dma_start(weights0[:], u0)
        nc.sync.dma_start(weights1[:], u1)

        clamped0 = held.tile([rows, n], F32, name="clamped0")
        clamped1 = held.tile([rows, n], F32, name="clamped1")
        product0 = held.tile([rows, n], F32, name="product0")
        product1 = held.tile([rows, n], F32, name="product1")
        total = held.tile([rows, n], F32, name="total")

        width = n // 2
        halves = (slice(0, width), slice(width, n))

        for half in halves:
            entries = offsets[:, half.start // 16 : half.stop // 16]
            nc.vector.tensor_scalar(clamped0[:, half], table[:].indirect(entries), LOW, HIGH, alu.max, alu.min)
            nc.gpsimd.tensor_tensor(product0[:, half], clamped0[:, half], weights0[:, half], alu.mult)

        for half in halves:
            entries = offsets[:, (n + half.start) // 16 : (n + half.stop) // 16]
            nc.vector.tensor_scalar(clamped1[:, half], table[:].indirect(entries), LOW, HIGH, alu.max, alu.min)
        for half in halves:
            nc.vector.tensor_tensor(product1[:, half], clamped1[:, half], weights1[:, half], alu.mult)
        for half in halves:
            nc.vector.tensor_tensor(total[:, half], product0[:, half], product1[:, half], alu.add)
        nc.sync.dma_start(out, total[:])
